import numpy as np
import ml_dtypes

BF16 = ml_dtypes.bfloat16


def bf(x):
    return np.asarray(x, np.float32).astype(BF16)


def f32(x):
    return np.asarray(x, np.float32)


def f64(x):
    return np.asarray(x).astype(np.float64)


def striped(idx):
    return np.tile(idx.reshape(-1, 16).T, (8, 1))


def rows(idx, k):
    return np.tile(idx, (k, 1))


def look(tab, idx):
    return np.take_along_axis(f64(tab), rows(idx, len(tab)), axis=1)


K, S, V, N, M = 128, 2048, 1536, 1536, 128


def setup_inputs():
    return {"tab": f32(np.random.standard_normal((2, K, S))), "y": f32(1.0 * np.random.standard_normal((K, V))), "w": bf(np.random.standard_normal((K, M)) / np.sqrt(K)), "b": f32(0.5 * np.random.standard_normal((M, 1))), "offs": striped(np.random.permutation(S)[:N])}


def reference(tab, y, w, b, offs):
    idx = offs[:16].T.reshape(-1)
    x = look(tab[0], idx) / (1.0 + np.exp(-look(tab[0], idx))) * f64(y) + look(tab[1], idx)
    return np.maximum(f64(w).T @ x + f64(b), 0.0)

@@ -1,0 +1,57 @@
+import concourse.mybir as mybir
+
+P = 128
+PLACES = 2048
+N = 1536
+M = 128
+ENTRIES_PER_COLUMN = 16
+GATE_PIECE = 512
+SUM_PIECE = 256
+
+FLOPS = 2 * P * M * N
+
+F32, BF16, U16 = mybir.dt.float32, mybir.dt.bfloat16, mybir.dt.uint16
+ACT, ALU = mybir.ActivationFunctionType, mybir.AluOpType
+
+
+def tile_lookup_resglu_relu_kernel(tc, tab, y, w, b, offs, out):
+    nc = tc.nc
+    with (
+        tc.tile_pool(name="held", bufs=1) as held,
+        tc.psum_pool(name="psum", bufs=1) as psum,
+    ):
+        offsets = held.tile([P, N // ENTRIES_PER_COLUMN], U16, name="offsets")
+        gates = held.tile([P, PLACES], F32, name="gates")
+        shifts = held.tile([P, PLACES], F32, name="shifts")
+        stream = held.tile([P, N], F32, name="stream")
+        weights = held.tile([P, M], BF16, name="weights")
+        bias = held.tile([M, 1], F32, name="bias")
+        silu = held.tile([P, N], F32, name="silu")
+        gated = held.tile([P, N], F32, name="gated")
+        x = held.tile([P, N], F32, name="x")
+        x_bf16 = held.tile([P, N], BF16, name="x_bf16")
+        result = held.tile([M, N], F32, name="result")
+
+        def entries(cols):
+            return offsets[:, cols.start // ENTRIES_PER_COLUMN : cols.stop // ENTRIES_PER_COLUMN]
+
+        nc.sync.dma_start(offsets[:], offs)
+        nc.sync.dma_start(gates[:], tab[0])
+        nc.sync.dma_start(stream[:], y)
+        nc.sync.dma_start(shifts[:], tab[1])
+        nc.sync.dma_start(weights[:], w)
+        nc.sync.dma_start(bias[:], b)
+
+        for start in range(0, N, GATE_PIECE):
+            cols = slice(start, start + GATE_PIECE)
+            nc.scalar.activation(silu[:, cols], gates[:].indirect(entries(cols)), ACT.Silu)
+            nc.vector.tensor_tensor(gated[:, cols], silu[:, cols], stream[:, cols], ALU.mult)
+
+        for start in range(0, N, SUM_PIECE):
+            cols = slice(start, start + SUM_PIECE)
+            nc.vector.tensor_tensor(x[:, cols], shifts[:].indirect(entries(cols)), gated[:, cols], ALU.add)
+            nc.scalar.copy(x_bf16[:, cols], x[:, cols])
+            product = psum.tile([M, SUM_PIECE], F32, name=f"product{start // SUM_PIECE}")
+            nc.tensor.matmul(product[:], weights[:], x_bf16[:, cols], start=True, stop=True)
+            nc.scalar.activation(result[:, cols], product[:], ACT.Relu, bias=bias[:])
+            nc.sync.dma_start(out[:, cols], result[:, cols])

@@ -35,6 +35,10 @@ def tile_lookup_resglu_relu_kernel(tc, tab, y, w, b, offs, out):
         def entries(cols):
             return offsets[:, cols.start // ENTRIES_PER_COLUMN : cols.stop // ENTRIES_PER_COLUMN]
 
+        warm = held.tile([P, 8], F32, name="warm")
+        nc.vector.memset(warm[:], 0.0)
+        nc.scalar.activation(warm[:], warm[:], ACT.Silu)
+
         nc.sync.dma_start(offsets[:], offs)
         nc.sync.dma_start(gates[:], tab[0])
         nc.sync.dma_start(stream[:], y)

@@ -39,23 +39,42 @@ def tile_lookup_resglu_relu_kernel(tc, tab, y, w, b, offs, out):
         nc.vector.memset(warm[:], 0.0)
         nc.scalar.activation(warm[:], warm[:], ACT.Silu)
 
-        nc.sync.dma_start(offsets[:], offs)
         nc.sync.dma_start(gates[:], tab[0])
-        nc.sync.dma_start(stream[:], y)
+        nc.sync.dma_start(offsets[:], offs)
+        nc.sync.dma_start(stream[:, :GATE_PIECE], y[:, :GATE_PIECE])
         nc.sync.dma_start(shifts[:], tab[1])
         nc.sync.dma_start(weights[:], w)
         nc.sync.dma_start(bias[:], b)
+        for start in range(GATE_PIECE, N, GATE_PIECE):
+            nc.sync.dma_start(stream[:, start : start + GATE_PIECE], y[:, start : start + GATE_PIECE])
 
         for start in range(0, N, GATE_PIECE):
             cols = slice(start, start + GATE_PIECE)
             nc.scalar.activation(silu[:, cols], gates[:].indirect(entries(cols)), ACT.Silu)
+
+        def gate_stream(start):
+            cols = slice(start, start + SUM_PIECE)
             nc.vector.tensor_tensor(gated[:, cols], silu[:, cols], stream[:, cols], ALU.mult)
 
-        for start in range(0, N, SUM_PIECE):
-            cols = slice(start, start + SUM_PIECE)
+        ahead = 2 * SUM_PIECE
+        for start in range(0, ahead, SUM_PIECE):
+            gate_stream(start)
+
+        starts = list(range(0, N, SUM_PIECE)) + [N - SUM_PIECE // 2]
+        for start, stop in zip(starts, starts[1:] + [N]):
+            cols = slice(start, stop)
+            last = stop == N
             nc.vector.tensor_tensor(x[:, cols], shifts[:].indirect(entries(cols)), gated[:, cols], ALU.add)
-            nc.scalar.copy(x_bf16[:, cols], x[:, cols])
-            product = psum.tile([M, SUM_PIECE], F32, name=f"product{start // SUM_PIECE}")
+            if start + ahead < N:
+                gate_stream(start + ahead)
+            if last:
+                nc.vector.tensor_copy(x_bf16[:, cols], x[:, cols])
+            else:
+                nc.scalar.copy(x_bf16[:, cols], x[:, cols])
+            product = psum.tile([M, stop - start], F32, name=f"product{start}")
             nc.tensor.matmul(product[:], weights[:], x_bf16[:, cols], start=True, stop=True)
-            nc.scalar.activation(result[:, cols], product[:], ACT.Relu, bias=bias[:])
+            if last:
+                nc.vector.tensor_scalar(result[:, cols], product[:], bias[:], 0.0, ALU.add, ALU.max)
+            else:
+                nc.scalar.activation(result[:, cols], product[:], ACT.Relu, bias=bias[:])
             nc.sync.dma_start(out[:, cols], result[:, cols])

@@ -52,29 +52,43 @@ def tile_lookup_resglu_relu_kernel(tc, tab, y, w, b, offs, out):
             cols = slice(start, start + GATE_PIECE)
             nc.scalar.activation(silu[:, cols], gates[:].indirect(entries(cols)), ACT.Silu)
 
-        def gate_stream(start):
-            cols = slice(start, start + SUM_PIECE)
+        def gate_stream(cols):
             nc.vector.tensor_tensor(gated[:, cols], silu[:, cols], stream[:, cols], ALU.mult)
 
-        ahead = 2 * SUM_PIECE
-        for start in range(0, ahead, SUM_PIECE):
-            gate_stream(start)
-
-        starts = list(range(0, N, SUM_PIECE)) + [N - SUM_PIECE // 2]
-        for start, stop in zip(starts, starts[1:] + [N]):
-            cols = slice(start, stop)
-            last = stop == N
+        def add_shifts(cols):
             nc.vector.tensor_tensor(x[:, cols], shifts[:].indirect(entries(cols)), gated[:, cols], ALU.add)
-            if start + ahead < N:
-                gate_stream(start + ahead)
-            if last:
-                nc.vector.tensor_copy(x_bf16[:, cols], x[:, cols])
-            else:
-                nc.scalar.copy(x_bf16[:, cols], x[:, cols])
-            product = psum.tile([M, stop - start], F32, name=f"product{start}")
+
+        def project(cols):
+            product = psum.tile([M, cols.stop - cols.start], F32, name=f"product{cols.start}")
             nc.tensor.matmul(product[:], weights[:], x_bf16[:, cols], start=True, stop=True)
-            if last:
-                nc.vector.tensor_scalar(result[:, cols], product[:], bias[:], 0.0, ALU.add, ALU.max)
-            else:
-                nc.scalar.activation(result[:, cols], product[:], ACT.Relu, bias=bias[:])
+            return product
+
+        def finish_on_scalar(product, cols):
+            nc.scalar.activation(result[:, cols], product[:], ACT.Relu, bias=bias[:])
             nc.sync.dma_start(out[:, cols], result[:, cols])
+
+        starts = list(range(0, N - GATE_PIECE, SUM_PIECE)) + list(range(N - GATE_PIECE, N, SUM_PIECE // 2))
+        pieces = [slice(start, stop) for start, stop in zip(starts, starts[1:] + [N])]
+        *body, before_last, last = pieces
+
+        ahead = 2
+        for cols in pieces[:ahead]:
+            gate_stream(cols)
+
+        products = []
+        for i, cols in enumerate(body):
+            add_shifts(cols)
+            gate_stream(pieces[i + ahead])
+            nc.scalar.copy(x_bf16[:, cols], x[:, cols])
+            products.append(project(cols))
+            if i > 0:
+                finish_on_scalar(products[i - 1], body[i - 1])
+
+        add_shifts(before_last)
+        add_shifts(last)
+        finish_on_scalar(products[-1], body[-1])
+        nc.vector.tensor_copy(x_bf16[:, before_last], x[:, before_last])
+        finish_on_scalar(project(before_last), before_last)
+        nc.vector.tensor_copy(x_bf16[:, last], x[:, last])
+        nc.vector.tensor_scalar(result[:, last], project(last)[:], bias[:], 0.0, ALU.add, ALU.max)
+        nc.sync.dma_start(out[:, last], result[:, last])

import concourse.mybir as mybir

P = 128
PLACES = 2048
N = 1536
M = 128
ENTRIES_PER_COLUMN = 16
GATE_PIECE = 512
SUM_PIECE = 256

FLOPS = 2 * P * M * N

F32, BF16, U16 = mybir.dt.float32, mybir.dt.bfloat16, mybir.dt.uint16
ACT, ALU = mybir.ActivationFunctionType, mybir.AluOpType


def tile_lookup_resglu_relu_kernel(tc, tab, y, w, b, offs, out):
    nc = tc.nc
    with (
        tc.tile_pool(name="held", bufs=1) as held,
        tc.psum_pool(name="psum", bufs=1) as psum,
    ):
        offsets = held.tile([P, N // ENTRIES_PER_COLUMN], U16, name="offsets")
        gates = held.tile([P, PLACES], F32, name="gates")
        shifts = held.tile([P, PLACES], F32, name="shifts")
        stream = held.tile([P, N], F32, name="stream")
        weights = held.tile([P, M], BF16, name="weights")
        bias = held.tile([M, 1], F32, name="bias")
        silu = held.tile([P, N], F32, name="silu")
        gated = held.tile([P, N], F32, name="gated")
        x = held.tile([P, N], F32, name="x")
        x_bf16 = held.tile([P, N], BF16, name="x_bf16")
        result = held.tile([M, N], F32, name="result")

        def entries(cols):
            return offsets[:, cols.start // ENTRIES_PER_COLUMN : cols.stop // ENTRIES_PER_COLUMN]

        warm = held.tile([P, 8], F32, name="warm")
        nc.vector.memset(warm[:], 0.0)
        nc.scalar.activation(warm[:], warm[:], ACT.Silu)

        nc.sync.dma_start(gates[:], tab[0])
        nc.sync.dma_start(offsets[:], offs)
        nc.sync.dma_start(stream[:, :GATE_PIECE], y[:, :GATE_PIECE])
        nc.sync.dma_start(shifts[:], tab[1])
        nc.sync.dma_start(weights[:], w)
        nc.sync.dma_start(bias[:], b)
        for start in range(GATE_PIECE, N, GATE_PIECE):
            nc.sync.dma_start(stream[:, start : start + GATE_PIECE], y[:, start : start + GATE_PIECE])

        for start in range(0, N, GATE_PIECE):
            cols = slice(start, start + GATE_PIECE)
            nc.scalar.activation(silu[:, cols], gates[:].indirect(entries(cols)), ACT.Silu)

        def gate_stream(cols):
            nc.vector.tensor_tensor(gated[:, cols], silu[:, cols], stream[:, cols], ALU.mult)

        def add_shifts(cols):
            nc.vector.tensor_tensor(x[:, cols], shifts[:].indirect(entries(cols)), gated[:, cols], ALU.add)

        def project(cols):
            product = psum.tile([M, cols.stop - cols.start], F32, name=f"product{cols.start}")
            nc.tensor.matmul(product[:], weights[:], x_bf16[:, cols], start=True, stop=True)
            return product

        def finish_on_scalar(product, cols):
            nc.scalar.activation(result[:, cols], product[:], ACT.Relu, bias=bias[:])
            nc.sync.dma_start(out[:, cols], result[:, cols])

        starts = list(range(0, N - GATE_PIECE, SUM_PIECE)) + list(range(N - GATE_PIECE, N, SUM_PIECE // 2))
        pieces = [slice(start, stop) for start, stop in zip(starts, starts[1:] + [N])]
        *body, before_last, last = pieces

        ahead = 2
        for cols in pieces[:ahead]:
            gate_stream(cols)

        products = []
        for i, cols in enumerate(body):
            add_shifts(cols)
            gate_stream(pieces[i + ahead])
            nc.scalar.copy(x_bf16[:, cols], x[:, cols])
            products.append(project(cols))
            if i > 0:
                finish_on_scalar(products[i - 1], body[i - 1])

        add_shifts(before_last)
        add_shifts(last)
        finish_on_scalar(products[-1], body[-1])
        nc.vector.tensor_copy(x_bf16[:, before_last], x[:, before_last])
        finish_on_scalar(project(before_last), before_last)
        nc.vector.tensor_copy(x_bf16[:, last], x[:, last])
        nc.vector.tensor_scalar(result[:, last], project(last)[:], bias[:], 0.0, ALU.add, ALU.max)
        nc.sync.dma_start(out[:, last], result[:, last])
